import numpy as np
import ml_dtypes


def mxq(x, axis, fmt="e4m3"):
    dtype, down = {"e4m3": (ml_dtypes.float8_e4m3fn, 7), "e5m2": (ml_dtypes.float8_e5m2, 14)}[fmt]
    v = np.moveaxis(np.asarray(x, np.float32).astype(ml_dtypes.bfloat16).astype(np.float64), axis, -1)
    blocks = v.reshape(v.shape[:-1] + (-1, 32))
    amax = np.abs(blocks).max(-1, keepdims=True)
    byte = np.maximum(np.where(amax > 0, np.frexp(amax)[1] - 1 + 127, 0) - down, 1)
    scale = np.exp2(byte - 127.0)
    codes = (blocks / scale).astype(np.float32).astype(dtype).astype(np.float64)
    return np.moveaxis((codes * scale).reshape(v.shape), -1, axis)


WIDE = False


def mx_kscale(k):
    if not WIDE:
        return np.ones(k)
    levels = np.array([10, -10, 5, -5, 0])
    if k % 512:
        return np.exp2(np.random.permutation(np.resize(levels, k // 32))).repeat(32)
    a = np.empty((k // 512, 16))
    for p in range(k // 512):
        a[p, :8] = np.random.permutation(np.resize(levels, 8))
        for g in range(8):
            far = levels[np.abs(levels - a[p, g]) >= 10]
            a[p, g + 8] = far[np.random.randint(len(far))]
    return np.exp2(a.ravel()).repeat(32)


def f64(x):
    return np.asarray(x).astype(np.float64)


def striped(idx):
    return np.tile(idx.reshape(-1, 16).T, (8, 1)).astype(np.uint16)


def unstriped(offs):
    return offs[:16].T.reshape(-1).astype(np.int64)


def striped8(idx):
    return np.concatenate([x.reshape(-1, 16).T for x in idx]).astype(np.uint16)


def runs(offs, k):
    lists = np.stack([offs[16 * r : 16 * r + 16].T.reshape(-1) for r in range(8)]).astype(np.int64)
    return lists[np.arange(k) % 512 // 64]


def pack_weight(w):
    k, n = w.shape
    w = f64(np.asarray(w, np.float32).astype(ml_dtypes.bfloat16)).reshape(k // 32, 32, n)
    amax = np.abs(w).max(1)
    byte = np.clip(np.where(amax > 0, np.frexp(amax)[1] - 1 + 127 - 7, 1), 1, 254)
    scaled = (w * np.exp2(127.0 - byte)[:, None, :]).reshape(k, n).astype(np.float32)
    words = np.ascontiguousarray(scaled.reshape(k // 512, 128, 4, n).transpose(0, 1, 3, 2)).astype(ml_dtypes.float8_e4m3fn).view(np.uint8)
    return words, np.ascontiguousarray(byte.astype(np.uint8).reshape(k // 512, 16, n))


def unpack_weight(words, scales):
    g, p, n, _ = words.shape
    vals = np.ascontiguousarray(words).view(ml_dtypes.float8_e4m3fn).astype(np.float64) * np.repeat(np.exp2(scales.astype(np.float64) - 127.0), 8, axis=1)[..., None]
    return vals.transpose(0, 1, 3, 2).reshape(g * 512, n)

def planes(y):
    n, m = y.shape
    v = y.astype(np.float32).astype(ml_dtypes.bfloat16).astype(np.float64).reshape(n // 32, 32, m)
    top = np.abs(v).max(1)
    byte = np.clip(np.where(top > 0, np.frexp(top)[1] - 1 + 127 - 7, 1), 1, 254)
    codes = (v * np.exp2(127.0 - byte)[:, None, :]).reshape(n, m).astype(np.float32).astype(ml_dtypes.float8_e4m3fn).view(np.uint8)
    words = codes.reshape(n // 512, 128, 4, m).transpose(0, 1, 3, 2)
    return np.ascontiguousarray(words), np.ascontiguousarray(byte.astype(np.uint8).reshape(n // 512, 16, m))


K, T, S, V, H, W = 512, 2048, 512, 512, 512, 256


def setup_inputs():
    n = np.random.standard_normal
    s = mx_kscale(K)[:, None]
    u = mx_kscale(S)
    packed_xT = pack_weight(n((K, T)) * s)
    packed_w1 = pack_weight(n((K, H)) / np.sqrt(K) / s)
    packed_w2 = pack_weight(n((K, H)) / np.sqrt(K) / s)
    perm = np.stack([np.random.permutation(V) for _ in range(8)])
    return {
        "x_words": packed_xT[0],
        "x_scales": packed_xT[1],
        "w1_words": packed_w1[0],
        "w1_scales": packed_w1[1],
        "w2_words": packed_w2[0],
        "w2_scales": packed_w2[1],
        "ga": (np.random.uniform(0.5, 1.5, (H, 1)) * u[:, None]).astype(np.float32),
        "gb": (np.random.uniform(0.5, 1.5, (H, 1)) / u[:, None]).astype(np.float32),
        "offs": striped(np.random.permutation(T)[:S]),
        "two": striped(np.random.permutation(T)[:V]),
        "n1": striped8(np.stack([np.random.permutation(S) for _ in range(8)])),
        "n2": striped8(np.stack([np.random.permutation(V) for _ in range(8)])),
        "n3": striped8(np.stack([np.random.permutation(V) for _ in range(8)])),
        "n4": striped8(np.stack([np.random.permutation(V) for _ in range(8)])),
        "n5": striped8(perm[:, :W]),
        "n6": striped8(perm[:, W:]),
        "n7": striped8(np.stack([np.random.permutation(V) for _ in range(8)])),
    }


def reference(x_words, x_scales, w1_words, w1_scales, w2_words, w2_scales, ga, gb, offs, two, n1, n2, n3, n4, n5, n6, n7):
    xq = unpack_weight(x_words, x_scales)[:, unstriped(offs)]
    a = unpack_weight(w1_words, w1_scales).T @ xq
    z = f64(ga) * (np.maximum(a, a[np.arange(H)[:, None], runs(n1, H)]))
    x_two = unpack_weight(x_words, x_scales)[:, unstriped(two)]
    b = unpack_weight(w2_words, w2_scales).T @ x_two
    z2 = f64(gb) * (b + b[np.arange(H)[:, None], runs(n2, H)] - (np.maximum(b[np.arange(H)[:, None], runs(n3, H)], b[np.arange(H)[:, None], runs(n4, H)])))
    s = 0.0625 * ((mxq(z, 0, "e4m3").T @ mxq(z2, 0, "e4m3")))
    pa = s[np.arange(S)[:, None], runs(n5, S)]
    pb = s[np.arange(S)[:, None], runs(n6, S)]
    ra = pa - (0.5 * pb)
    ds = s.copy()
    ds[np.arange(S)[:, None], runs(n6, S)] = ra
    out_0 = ds - (0.5 * (ds[np.arange(S)[:, None], runs(n7, S)]))
    return (out_0,) + planes(out_0)

@@ -1,0 +1,299 @@
+from contextlib import ExitStack
+
+import concourse.mybir as mybir
+from concourse.masks import make_identity
+
+F32 = mybir.dt.float32
+BF16 = mybir.dt.bfloat16
+I32 = mybir.dt.int32
+U32 = mybir.dt.uint32
+U16 = mybir.dt.uint16
+U8 = mybir.dt.uint8
+FP8X4 = mybir.dt.float8_e4m3fn_x4
+ALU = mybir.AluOpType
+ACT = mybir.ActivationFunctionType
+
+P = 128
+PACK = 4
+T = 2048
+D = 512
+GROUP = 16
+FLOPS = 3 * 2 * D * D * D
+S_SCALE = 0.0625
+HALF_BIG = 2.0**126
+
+
+def tile_picked_kqbigtrimfoldd_none_po_kernel(
+    tc, x_words, x_scales, w1_words, w1_scales, w2_words, w2_scales, ga, gb, offs, two, n1, n2, n3, n4, n5, n6, n7, out_0, out_1, out_2
+):
+    nc = tc.nc
+    with ExitStack() as ctx:
+        keep = ctx.enter_context(tc.tile_pool(name="keep", bufs=1))
+        psum = ctx.enter_context(tc.psum_pool(name="psum", bufs=1))
+
+        def load_list(name, src):
+            tile = keep.tile(list(src.shape), U16, name=name)
+            nc.sync.dma_start(tile[:], src)
+            return tile
+
+        def entries(lst, c0, c1):
+            return lst[:, c0 // GROUP : c1 // GROUP]
+
+        def load_words(name, src, width):
+            tile = keep.tile([P, width], I32, name=name, align_bytes=64)
+            nc.sync.dma_start(tile[:], src[0].rearrange("p n t -> p (n t)").bitcast(I32))
+            return tile
+
+        def cleared_plane(engine, name, width):
+            tile = keep.tile([P, width], U8, name=name, align_bytes=64)
+            engine.memset(tile[:].bitcast(I32), 0)
+            return tile
+
+        def load_plane(queue, tile, src):
+            for q in range(4):
+                queue.dma_start(tile[32 * q : 32 * q + 4, :].bitcast(I32), src[0, 4 * q : 4 * q + 4, :].bitcast(I32))
+
+        def load_gain(name, src):
+            tile = keep.tile([P, PACK], F32, name=name)
+            nc.sync.dma_start(tile[:], src.rearrange("(p t) o -> p (t o)", t=PACK))
+            return tile
+
+        x_plane = cleared_plane(nc.gpsimd, "x_plane", T)
+        w2_plane = cleared_plane(nc.vector, "w2_plane", D)
+        w1_plane = cleared_plane(nc.vector, "w1_plane", D)
+        load_plane(nc.scalar, x_plane, x_scales)
+        two_l = load_list("two_l", two)
+        x_codes = load_words("x_codes", x_words, T)
+        offs_l = load_list("offs_l", offs)
+        w2_raw = load_words("w2_raw", w2_words, D)
+        load_plane(nc.scalar, w2_plane, w2_scales)
+        gb_t = load_gain("gb_t", gb)
+        n3_l = load_list("n3_l", n3)
+        n4_l = load_list("n4_l", n4)
+        n2_l = load_list("n2_l", n2)
+        ga_t = load_gain("ga_t", ga)
+        w1_raw = load_words("w1_raw", w1_words, D)
+        load_plane(nc.sync, w1_plane, w1_scales)
+        n1_l = load_list("n1_l", n1)
+        n5_l = load_list("n5_l", n5)
+        n6_l = load_list("n6_l", n6)
+        n7_l = load_list("n7_l", n7)
+
+        ident = keep.tile([P, P], F32, name="ident")
+        make_identity(nc, ident[:])
+
+        def pick_plane(name, lst):
+            tile = keep.tile([P, D], U8, name=name, align_bytes=64)
+            nc.vector.tensor_copy(tile[:], x_plane[:].indirect(lst[:]))
+            return tile
+
+        def pick_codes(name, lst):
+            tile = keep.tile([P, D], U32, name=name, align_bytes=64)
+            nc.vector.tensor_copy(tile[:], x_codes[:].bitcast(U32).indirect(lst[:]))
+            return tile
+
+        def deal(name, raw, plane):
+            codes = keep.tile([P, D], I32, name=name + "_codes", align_bytes=64)
+            nc.vector.tensor_copy(
+                codes[:].rearrange("p (t m i) -> p m t i", t=PACK, i=4), raw[:].rearrange("p (m i t) -> p m t i", t=PACK, i=4)
+            )
+            scales = keep.tile([P, D], U8, name=name + "_scales", align_bytes=64)
+            nc.vector.tensor_copy(
+                scales[:].rearrange("p (t m i) -> p m t i", t=PACK, i=16), plane[:].rearrange("p (m i t) -> p m t i", t=PACK, i=16)
+            )
+            return codes, scales
+
+        def mx(out, lhs, t, rhs):
+            cols = slice(P * t, P * (t + 1))
+            nc.tensor.matmul_mx(
+                out=out, lhsT=lhs[0][:, cols].bitcast(FP8X4), lhsT_scale=lhs[1][:, cols],
+                rhs=rhs[0][:].bitcast(FP8X4), rhs_scale=rhs[1][:], start=True, stop=True,
+            )
+
+        flip = keep.tile([P, PACK], F32, name="flip")
+        nc.scalar.activation(flip[:], gb_t[:], ACT.Sign, scale=-1.0)
+        gb_abs = keep.tile([P, PACK], F32, name="gb_abs")
+        nc.scalar.activation(gb_abs[:], gb_t[:], ACT.Abs)
+        b_gain = keep.tile([P, PACK], F32, name="b_gain")
+        nc.scalar.activation(b_gain[:], gb_abs[:], ACT.Copy, scale=-1.0)
+        a_gain = keep.tile([P, PACK], F32, name="a_gain")
+        for t in range(PACK):
+            nc.scalar.activation(a_gain[:, t : t + 1], ga_t[:, t : t + 1], ACT.Copy, scale=flip[:, t : t + 1])
+        a_sign = keep.tile([P, PACK], F32, name="a_sign")
+        nc.scalar.activation(a_sign[:], a_gain[:], ACT.Sign)
+        a_low = keep.tile([P, PACK], F32, name="a_low")
+        nc.scalar.activation(a_low[:], a_sign[:], ACT.Copy, scale=HALF_BIG, bias=-HALF_BIG)
+        a_high = keep.tile([P, PACK], F32, name="a_high")
+        nc.scalar.activation(a_high[:], a_sign[:], ACT.Copy, scale=HALF_BIG, bias=HALF_BIG)
+
+        two_plane = pick_plane("two_plane", two_l)
+        offs_plane = pick_plane("offs_plane", offs_l)
+        w2 = deal("w2", w2_raw, w2_plane)
+        two_codes = pick_codes("two_codes", two_l)
+        LAST = slice(384, 512)
+        b_rows, b_last = [], []
+        for t in range(PACK):
+            acc = psum.tile([P, D], F32, name="prod", tag="prod", bufs=4)
+            mx(acc[:], w2, t, (two_codes, two_plane))
+            row = keep.tile([P, D], F32, name="b_row%d" % t)
+            nc.scalar.activation(row[:], acc[:], ACT.Copy, scale=b_gain[:, t : t + 1])
+            last = keep.tile([P, P], F32, name="b_last%d" % t)
+            nc.scalar.activation(last[:], acc[:, LAST], ACT.Copy, scale=b_gain[:, t : t + 1])
+            b_rows.append(row)
+            b_last.append(last)
+        offs_codes = pick_codes("offs_codes", offs_l)
+        w1 = deal("w1", w1_raw, w1_plane)
+        a_rows, a_again = [], []
+        for t in range(PACK):
+            acc = psum.tile([P, D], F32, name="prod", tag="prod", bufs=4)
+            mx(acc[:], w1, t, (offs_codes, offs_plane))
+            row = keep.tile([P, D], F32, name="a_row%d" % t)
+            nc.scalar.activation(row[:], acc[:], ACT.Copy, scale=a_gain[:, t : t + 1])
+            again = keep.tile([P, D], F32, name="a_again%d" % t)
+            nc.sync.dma_start(again[:], row[:])
+            a_rows.append(row)
+            a_again.append(again)
+
+        def sum_and_turn(name, terms, width):
+            back = psum.tile([P, 2, width], F32, name="back", tag="back", bufs=2)
+            for c in range(width // P):
+                cols = slice(P * c, P * (c + 1))
+                total = psum.tile([P, PACK, P], F32, name="total", tag="total", bufs=2)
+                for t in range(PACK):
+                    for i, term in enumerate(terms[t]):
+                        nc.tensor.matmul(total[:, t, :], term[:, cols], ident[:], start=(i == 0), stop=(i == len(terms[t]) - 1), is_transpose=True)
+                turned = keep.tile([P, 2, 2 * P], BF16, name="turned", tag="turned", bufs=3)
+                nc.scalar.activation(
+                    turned[:].rearrange("j u (p e) -> j u p e", e=2), total[:].rearrange("j (u e) p -> j u p e", e=2), ACT.Copy
+                )
+                for u in range(2):
+                    nc.tensor.transpose(back[:, u, cols], turned[:, u, :].bitcast(F32), ident[:])
+            return back
+
+        def quantise(name, src, width):
+            codes = keep.tile([P, width], U32, name=name + "_codes", align_bytes=64)
+            scales = keep.tile([P, width], U8, name=name + "_scales", align_bytes=64)
+            nc.vector.quantize_mx(out=codes[:].bitcast(FP8X4), scales=scales[:], in_=src)
+            return codes, scales
+
+        def b_chunk(name, c0, c1, tag):
+            width = c1 - c0
+            g3 = keep.tile([P, PACK, width], F32, name=name + "_g3", tag=tag)
+            d = keep.tile([P, PACK, width], F32, name=name + "_d")
+            e = keep.tile([P, PACK, width], F32, name=name + "_e")
+            r = keep.tile([P, PACK, width], F32, name=name + "_r")
+            for t in range(PACK + 1):
+                if t < PACK:
+                    nc.vector.tensor_copy(g3[:, t, :], b_rows[t][:].indirect(entries(n3_l, c0, c1)))
+                if t > 0:
+                    s = t - 1
+                    nc.vector.tensor_tensor(d[:, s, :], b_rows[s][:].indirect(entries(n4_l, c0, c1)), g3[:, s, :], ALU.subtract)
+                    nc.scalar.activation(r[:, s, :], d[:, s, :], ACT.Relu, scale=-1.0)
+                    nc.vector.tensor_tensor(e[:, s, :], b_rows[s][:].indirect(entries(n2_l, c0, c1)), g3[:, s, :], ALU.subtract)
+            back = sum_and_turn(name, [[b_rows[t][:, c0:c1], r[:, t, :], e[:, t, :]] for t in range(PACK)], width)
+            packed = keep.tile([P, PACK * width], BF16, name=name + "_packed", tag=name + "_packed", align_bytes=64)
+            nc.scalar.copy(packed[:].bitcast(F32).rearrange("p (j u) -> p j u", u=2), back[:].rearrange("p u j -> p j u"))
+            return packed
+
+        z_packed = keep.tile([P, PACK * D], BF16, name="z_packed", tag="z_packed", align_bytes=64)
+
+        def a_chunk(name, c0, c1, tag):
+            width = c1 - c0
+            d = keep.tile([P, PACK, width], F32, name=name + "_d", tag=tag)
+            signed = keep.tile([P, PACK, width], F32, name=name + "_signed")
+            for t in range(PACK + 1):
+                if t < PACK:
+                    nc.vector.tensor_tensor(d[:, t, :], a_rows[t][:].indirect(entries(n1_l, c0, c1)), a_again[t][:, c0:c1], ALU.subtract)
+                if t > 0:
+                    s = t - 1
+                    nc.vector.tensor_scalar(signed[:, s, :], d[:, s, :], a_low[:, s : s + 1], a_high[:, s : s + 1], ALU.max, ALU.min)
+            back = sum_and_turn(name, [[a_rows[t][:, c0:c1], signed[:, t, :]] for t in range(PACK)], width)
+            words = z_packed[:].bitcast(F32).rearrange("p (t m u) -> p t m u", t=PACK, u=2)
+            nc.scalar.copy(words[:, :, c0 // PACK : c1 // PACK, :], back[:].rearrange("p u (m t) -> p t m u", t=PACK))
+
+        b0_packed = b_chunk("b0", 0, 256, "b0")
+        a_chunk("a0", 0, 256, "early")
+        a_chunk("a1", 256, 512, "late")
+        z2_0 = quantise("z2_0", b0_packed[:], 256)
+        b1_packed = b_chunk("b1", 256, 384, "early")
+
+        both = keep.tile([P, PACK, P], F32, name="both", tag="late")
+        m3 = keep.tile([P, PACK, P], F32, name="m3")
+        for t in range(PACK):
+            nc.vector.tensor_tensor(both[:, t, :], b_rows[t][:].indirect(entries(n2_l, 384, 512)), b_last[t][:], ALU.add)
+        for t in range(PACK):
+            nc.vector.tensor_tensor(m3[:, t, :], b_rows[t][:].indirect(entries(n3_l, 384, 512)), both[:, t, :], ALU.subtract)
+        z = quantise("z", z_packed[:], D)
+        m4 = keep.tile([P, PACK, P], F32, name="m4", tag="z_packed", align_bytes=64)
+        for t in range(PACK):
+            nc.vector.tensor_tensor(m4[:, t, :], b_rows[t][:].indirect(entries(n4_l, 384, 512)), both[:, t, :], ALU.subtract)
+        z2_1 = quantise("z2_1", b1_packed[:], P)
+        b2_packed = keep.tile([P, PACK * P], BF16, name="b2_packed", tag="b1_packed", align_bytes=64)
+        nc.vector.tensor_tensor(
+            b2_packed[:].rearrange("p (c i t) -> p c t i", t=PACK, i=4),
+            m3[:].rearrange("p t (c i) -> p c t i", i=4), m4[:].rearrange("p t (c i) -> p c t i", i=4), ALU.min,
+        )
+
+        s_acc, ds = [], []
+        for t in range(PACK):
+            acc = psum.tile([P, D], F32, name="prod", tag="prod", bufs=4)
+            mx(acc[:, 0:256], z, t, z2_0)
+            mx(acc[:, 256:384], z, t, z2_1)
+            row = keep.tile([P, D], F32, name="ds%d" % t)
+            s_acc.append(acc)
+            ds.append(row)
+        nc.scalar.activation(ds[0][:, 0:384], s_acc[0][:, 0:384], ACT.Copy, scale=S_SCALE)
+        z2_2 = quantise("z2_2", b2_packed[:], P)
+        for t in range(PACK):
+            mx(s_acc[t][:, LAST], z, t, z2_2)
+            if t > 0:
+                nc.scalar.activation(ds[t][:, 0:384], s_acc[t][:, 0:384], ACT.Copy, scale=S_SCALE)
+            nc.scalar.activation(ds[t][:, LAST], s_acc[t][:, LAST], ACT.Copy, scale=-S_SCALE)
+
+        pa = keep.tile([P, PACK, D // 2], F32, name="pa")
+        pb = keep.tile([P, PACK, D // 2], F32, name="pb")
+        halves = []
+        for t in range(PACK + 1):
+            if t < PACK:
+                nc.vector.tensor_copy(pa[:, t, :], ds[t][:].indirect(n5_l[:]))
+                nc.vector.tensor_scalar(pb[:, t, :], ds[t][:].indirect(n6_l[:]), -0.5, 0.0, ALU.mult, ALU.add)
+            if t > 0:
+                s = t - 1
+                nc.vector.tensor_tensor(ds[s][:].indirect(n6_l[:]), pa[:, s, :], pb[:, s, :], ALU.add)
+                half = keep.tile([P, D], F32, name="half%d" % s)
+                nc.scalar.activation(half[:], ds[s][:], ACT.Copy, scale=-0.5)
+                halves.append(half)
+
+        out_rows = out_0.rearrange("(p t) v -> p t v", t=PACK)
+        out_words = out_1[0].rearrange("p n t -> p (n t)").bitcast(I32)
+        o_codes = keep.tile([P, D], U32, name="o_codes", align_bytes=64)
+        o_plane = keep.tile([P, D], U8, name="o_plane", align_bytes=64)
+        chunks = [(0, 256), (256, 384), (384, 512)]
+        results, packs = [], []
+        for c0, c1 in chunks:
+            width = c1 - c0
+            res = keep.tile([P, PACK, width], F32, name="res%d" % c0)
+            for t in range(PACK):
+                nc.vector.tensor_tensor(res[:, t, :], halves[t][:].indirect(entries(n7_l, c0, c1)), ds[t][:, c0:c1], ALU.add)
+            nc.sync.dma_start(out_rows[:, :, c0:c1], res[:])
+            results.append(res)
+            if c1 < D:
+                packed = keep.tile([P, PACK * width], BF16, name="res_packed", tag="res_packed%d" % c0, align_bytes=64)
+                nc.scalar.copy(packed[:].rearrange("p (c i t) -> p c t i", t=PACK, i=4), res[:].rearrange("p t (c i) -> p c t i", i=4))
+                packs.append(packed)
+
+        def quantise_out(i):
+            c0, c1 = chunks[i]
+            nc.vector.quantize_mx(out=o_codes[:, c0:c1].bitcast(FP8X4), scales=o_plane[:, c0:c1], in_=packs[i][:])
+
+        quantise_out(0)
+        packed = keep.tile([P, PACK * P], BF16, name="res_packed", tag="res_packed0", align_bytes=64)
+        nc.vector.tensor_copy(packed[:].rearrange("p (c i t) -> p c t i", t=PACK, i=4), results[2][:].rearrange("p t (c i) -> p c t i", i=4))
+        packs.append(packed)
+        quantise_out(1)
+        nc.sync.dma_start(out_words[:, 0:384], o_codes[:, 0:384].bitcast(I32))
+        quantise_out(2)
+        nc.scalar.dma_start(out_words[:, 384:512], o_codes[:, 384:512].bitcast(I32))
+        for q in range(4):
+            queue = nc.sync if q % 2 == 0 else nc.scalar
+            queue.dma_start(out_2[0, 4 * q : 4 * q + 4, :].bitcast(I32), o_plane[32 * q : 32 * q + 4, :].bitcast(I32))

@@ -18,6 +18,7 @@ PACK = 4
 T = 2048
 D = 512
 GROUP = 16
+HALF = D // 2
 FLOPS = 3 * 2 * D * D * D
 S_SCALE = 0.0625
 HALF_BIG = 2.0**126
@@ -44,9 +45,10 @@ def tile_picked_kqbigtrimfoldd_none_po_kernel(
             nc.sync.dma_start(tile[:], src[0].rearrange("p n t -> p (n t)").bitcast(I32))
             return tile
 
-        def cleared_plane(engine, name, width):
-            tile = keep.tile([P, width], U8, name=name, align_bytes=64)
-            engine.memset(tile[:].bitcast(I32), 0)
+        def cleared_plane(name, width):
+            tile = keep.tile([P, width], U8, name=name, tag=name, align_bytes=64)
+            nc.vector.memset(tile[:, 0 : width // 2].bitcast(I32), 0)
+            nc.gpsimd.memset(tile[:, width // 2 : width].bitcast(I32), 0)
             return tile
 
         def load_plane(queue, tile, src):
@@ -58,15 +60,15 @@ def tile_picked_kqbigtrimfoldd_none_po_kernel(
             nc.sync.dma_start(tile[:], src.rearrange("(p t) o -> p (t o)", t=PACK))
             return tile
 
-        x_plane = cleared_plane(nc.gpsimd, "x_plane", T)
-        w2_plane = cleared_plane(nc.vector, "w2_plane", D)
-        w1_plane = cleared_plane(nc.vector, "w1_plane", D)
-        load_plane(nc.scalar, x_plane, x_scales)
+        x_plane = cleared_plane("x_plane", T)
+        w2_plane = cleared_plane("w2_plane", D)
+        w1_plane = cleared_plane("w1_plane", D)
         two_l = load_list("two_l", two)
-        x_codes = load_words("x_codes", x_words, T)
         offs_l = load_list("offs_l", offs)
         w2_raw = load_words("w2_raw", w2_words, D)
-        load_plane(nc.scalar, w2_plane, w2_scales)
+        load_plane(nc.sync, x_plane, x_scales)
+        x_codes = load_words("x_codes", x_words, T)
+        load_plane(nc.sync, w2_plane, w2_scales)
         gb_t = load_gain("gb_t", gb)
         n3_l = load_list("n3_l", n3)
         n4_l = load_list("n4_l", n4)
@@ -87,8 +89,8 @@ def tile_picked_kqbigtrimfoldd_none_po_kernel(
             nc.vector.tensor_copy(tile[:], x_plane[:].indirect(lst[:]))
             return tile
 
-        def pick_codes(name, lst):
-            tile = keep.tile([P, D], U32, name=name, align_bytes=64)
+        def pick_codes(name, lst, tag):
+            tile = keep.tile([P, D], U32, name=name, tag=tag, align_bytes=64)
             nc.vector.tensor_copy(tile[:], x_codes[:].bitcast(U32).indirect(lst[:]))
             return tile
 
@@ -128,46 +130,43 @@ def tile_picked_kqbigtrimfoldd_none_po_kernel(
 
         two_plane = pick_plane("two_plane", two_l)
         offs_plane = pick_plane("offs_plane", offs_l)
+        two_codes = pick_codes("two_codes", two_l, "two_codes")
         w2 = deal("w2", w2_raw, w2_plane)
-        two_codes = pick_codes("two_codes", two_l)
-        LAST = slice(384, 512)
+        LAST = slice(HALF, D)
         b_rows, b_last = [], []
         for t in range(PACK):
-            acc = psum.tile([P, D], F32, name="prod", tag="prod", bufs=4)
+            acc = psum.tile([P, D], F32, name="prod", tag="prod", bufs=2)
             mx(acc[:], w2, t, (two_codes, two_plane))
             row = keep.tile([P, D], F32, name="b_row%d" % t)
             nc.scalar.activation(row[:], acc[:], ACT.Copy, scale=b_gain[:, t : t + 1])
-            last = keep.tile([P, P], F32, name="b_last%d" % t)
-            nc.scalar.activation(last[:], acc[:, LAST], ACT.Copy, scale=b_gain[:, t : t + 1])
             b_rows.append(row)
-            b_last.append(last)
-        offs_codes = pick_codes("offs_codes", offs_l)
+        offs_codes = pick_codes("offs_codes", offs_l, "w2_plane")
         w1 = deal("w1", w1_raw, w1_plane)
-        a_rows, a_again = [], []
+        a_wide = [keep.tile([P, 2 * D], F32, name="a_wide%d" % t) for t in range(PACK)]
         for t in range(PACK):
-            acc = psum.tile([P, D], F32, name="prod", tag="prod", bufs=4)
+            acc = psum.tile([P, D], F32, name="prod", tag="prod", bufs=2)
             mx(acc[:], w1, t, (offs_codes, offs_plane))
-            row = keep.tile([P, D], F32, name="a_row%d" % t)
-            nc.scalar.activation(row[:], acc[:], ACT.Copy, scale=a_gain[:, t : t + 1])
-            again = keep.tile([P, D], F32, name="a_again%d" % t)
-            nc.sync.dma_start(again[:], row[:])
-            a_rows.append(row)
-            a_again.append(again)
+            nc.scalar.activation(a_wide[t][:, 0:D], acc[:], ACT.Copy, scale=a_gain[:, t : t + 1])
+            nc.scalar.activation(a_wide[t ^ 1][:, D : 2 * D], acc[:], ACT.Copy, scale=a_gain[:, t : t + 1])
+        for t in range(PACK):
+            last = keep.tile([P, HALF], F32, name="b_last%d" % t)
+            nc.scalar.copy(last[:], b_rows[t][:, LAST])
+            b_last.append(last)
 
-        def sum_and_turn(name, terms, width):
-            back = psum.tile([P, 2, width], F32, name="back", tag="back", bufs=2)
-            for c in range(width // P):
-                cols = slice(P * c, P * (c + 1))
-                total = psum.tile([P, PACK, P], F32, name="total", tag="total", bufs=2)
+        def sum_and_turn(terms, c0):
+            back = psum.tile([P, 2, HALF], F32, name="back", tag="back", bufs=2)
+            for c in range(HALF // P):
+                cols = slice(c0 + P * c, c0 + P * (c + 1))
+                total = psum.tile([P, PACK, P], F32, name="total", tag="total", bufs=4)
                 for t in range(PACK):
                     for i, term in enumerate(terms[t]):
                         nc.tensor.matmul(total[:, t, :], term[:, cols], ident[:], start=(i == 0), stop=(i == len(terms[t]) - 1), is_transpose=True)
-                turned = keep.tile([P, 2, 2 * P], BF16, name="turned", tag="turned", bufs=3)
+                turned = keep.tile([P, 2, 2 * P], BF16, name="turned", tag="turned", bufs=4)
                 nc.scalar.activation(
                     turned[:].rearrange("j u (p e) -> j u p e", e=2), total[:].rearrange("j (u e) p -> j u p e", e=2), ACT.Copy
                 )
                 for u in range(2):
-                    nc.tensor.transpose(back[:, u, cols], turned[:, u, :].bitcast(F32), ident[:])
+                    nc.tensor.transpose(back[:, u, P * c : P * (c + 1)], turned[:, u, :].bitcast(F32), ident[:])
             return back
 
         def quantise(name, src, width):
@@ -176,79 +175,77 @@ def tile_picked_kqbigtrimfoldd_none_po_kernel(
             nc.vector.quantize_mx(out=codes[:].bitcast(FP8X4), scales=scales[:], in_=src)
             return codes, scales
 
-        def b_chunk(name, c0, c1, tag):
-            width = c1 - c0
-            g3 = keep.tile([P, PACK, width], F32, name=name + "_g3", tag=tag)
-            d = keep.tile([P, PACK, width], F32, name=name + "_d")
-            e = keep.tile([P, PACK, width], F32, name=name + "_e")
-            r = keep.tile([P, PACK, width], F32, name=name + "_r")
-            for t in range(PACK + 1):
-                if t < PACK:
-                    nc.vector.tensor_copy(g3[:, t, :], b_rows[t][:].indirect(entries(n3_l, c0, c1)))
-                if t > 0:
-                    s = t - 1
-                    nc.vector.tensor_tensor(d[:, s, :], b_rows[s][:].indirect(entries(n4_l, c0, c1)), g3[:, s, :], ALU.subtract)
-                    nc.scalar.activation(r[:, s, :], d[:, s, :], ACT.Relu, scale=-1.0)
-                    nc.vector.tensor_tensor(e[:, s, :], b_rows[s][:].indirect(entries(n2_l, c0, c1)), g3[:, s, :], ALU.subtract)
-            back = sum_and_turn(name, [[b_rows[t][:, c0:c1], r[:, t, :], e[:, t, :]] for t in range(PACK)], width)
-            packed = keep.tile([P, PACK * width], BF16, name=name + "_packed", tag=name + "_packed", align_bytes=64)
-            nc.scalar.copy(packed[:].bitcast(F32).rearrange("p (j u) -> p j u", u=2), back[:].rearrange("p u j -> p j u"))
-            return packed
-
-        z_packed = keep.tile([P, PACK * D], BF16, name="z_packed", tag="z_packed", align_bytes=64)
-
-        def a_chunk(name, c0, c1, tag):
-            width = c1 - c0
-            d = keep.tile([P, PACK, width], F32, name=name + "_d", tag=tag)
-            signed = keep.tile([P, PACK, width], F32, name=name + "_signed")
-            for t in range(PACK + 1):
-                if t < PACK:
-                    nc.vector.tensor_tensor(d[:, t, :], a_rows[t][:].indirect(entries(n1_l, c0, c1)), a_again[t][:, c0:c1], ALU.subtract)
-                if t > 0:
-                    s = t - 1
-                    nc.vector.tensor_scalar(signed[:, s, :], d[:, s, :], a_low[:, s : s + 1], a_high[:, s : s + 1], ALU.max, ALU.min)
-            back = sum_and_turn(name, [[a_rows[t][:, c0:c1], signed[:, t, :]] for t in range(PACK)], width)
-            words = z_packed[:].bitcast(F32).rearrange("p (t m u) -> p t m u", t=PACK, u=2)
-            nc.scalar.copy(words[:, :, c0 // PACK : c1 // PACK, :], back[:].rearrange("p u (m t) -> p t m u", t=PACK))
-
-        b0_packed = b_chunk("b0", 0, 256, "b0")
-        a_chunk("a0", 0, 256, "early")
-        a_chunk("a1", 256, 512, "late")
-        z2_0 = quantise("z2_0", b0_packed[:], 256)
-        b1_packed = b_chunk("b1", 256, 384, "early")
-
-        both = keep.tile([P, PACK, P], F32, name="both", tag="late")
-        m3 = keep.tile([P, PACK, P], F32, name="m3")
-        for t in range(PACK):
-            nc.vector.tensor_tensor(both[:, t, :], b_rows[t][:].indirect(entries(n2_l, 384, 512)), b_last[t][:], ALU.add)
-        for t in range(PACK):
-            nc.vector.tensor_tensor(m3[:, t, :], b_rows[t][:].indirect(entries(n3_l, 384, 512)), both[:, t, :], ALU.subtract)
-        z = quantise("z", z_packed[:], D)
-        m4 = keep.tile([P, PACK, P], F32, name="m4", tag="z_packed", align_bytes=64)
-        for t in range(PACK):
-            nc.vector.tensor_tensor(m4[:, t, :], b_rows[t][:].indirect(entries(n4_l, 384, 512)), both[:, t, :], ALU.subtract)
-        z2_1 = quantise("z2_1", b1_packed[:], P)
-        b2_packed = keep.tile([P, PACK * P], BF16, name="b2_packed", tag="b1_packed", align_bytes=64)
-        nc.vector.tensor_tensor(
-            b2_packed[:].rearrange("p (c i t) -> p c t i", t=PACK, i=4),
-            m3[:].rearrange("p t (c i) -> p c t i", i=4), m4[:].rearrange("p t (c i) -> p c t i", i=4), ALU.min,
-        )
-
-        s_acc, ds = [], []
-        for t in range(PACK):
-            acc = psum.tile([P, D], F32, name="prod", tag="prod", bufs=4)
-            mx(acc[:, 0:256], z, t, z2_0)
-            mx(acc[:, 256:384], z, t, z2_1)
-            row = keep.tile([P, D], F32, name="ds%d" % t)
-            s_acc.append(acc)
-            ds.append(row)
-        nc.scalar.activation(ds[0][:, 0:384], s_acc[0][:, 0:384], ACT.Copy, scale=S_SCALE)
-        z2_2 = quantise("z2_2", b2_packed[:], P)
-        for t in range(PACK):
-            mx(s_acc[t][:, LAST], z, t, z2_2)
+        g3_pairs = [keep.tile([P, 2, HALF], F32, name="g3", tag=tag, align_bytes=64) for tag in ("g3", "w1_plane")]
+        g3 = [g3_pairs[t // 2][:, t % 2, :] for t in range(PACK)]
+        d43 = keep.tile([P, PACK, HALF], F32, name="d43")
+        d23 = keep.tile([P, PACK, HALF], F32, name="d23")
+        r34 = keep.tile([P, PACK, HALF], F32, name="r34")
+        for t in range(PACK + 1):
+            if t < PACK:
+                nc.vector.tensor_copy(g3[t], b_rows[t][:].indirect(entries(n3_l, 0, HALF)))
             if t > 0:
-                nc.scalar.activation(ds[t][:, 0:384], s_acc[t][:, 0:384], ACT.Copy, scale=S_SCALE)
-            nc.scalar.activation(ds[t][:, LAST], s_acc[t][:, LAST], ACT.Copy, scale=-S_SCALE)
+                s = t - 1
+                nc.vector.tensor_tensor(d43[:, s, :], b_rows[s][:].indirect(entries(n4_l, 0, HALF)), g3[s], ALU.subtract)
+                nc.scalar.activation(r34[:, s, :], d43[:, s, :], ACT.Relu, scale=-1.0)
+                nc.vector.tensor_tensor(d23[:, s, :], b_rows[s][:].indirect(entries(n2_l, 0, HALF)), g3[s], ALU.subtract)
+        back = sum_and_turn([[b_rows[t][:], r34[:, t, :], d23[:, t, :]] for t in range(PACK)], 0)
+        y_first = keep.tile([P, PACK * HALF], BF16, name="y_first", tag="y_first", align_bytes=64)
+        nc.scalar.copy(y_first[:].bitcast(F32).rearrange("p (j u) -> p j u", u=2), back[:].rearrange("p u j -> p j u"))
+
+        steps, clamped = [], []
+        for t in range(PACK + 1):
+            if t < PACK:
+                step = keep.tile([P, D], F32, name="step", tag="step%d" % t)
+                nc.vector.tensor_tensor(step[:], a_wide[t][:].indirect(n1_l[:]), a_wide[t ^ 1][:, D : 2 * D], ALU.subtract)
+                steps.append(step)
+            if t > 0:
+                s = t - 1
+                kept = keep.tile([P, D], F32, name="clamped%d" % s)
+                nc.vector.tensor_scalar(kept[:], steps[s][:], a_low[:, s : s + 1], a_high[:, s : s + 1], ALU.max, ALU.min)
+                clamped.append(kept)
+        z_packed = keep.tile([P, PACK * D], BF16, name="z_packed", tag="z_packed", align_bytes=64)
+        z_words = z_packed[:].bitcast(F32).rearrange("p (t m u) -> p t m u", t=PACK, u=2)
+        for c0 in (0, HALF):
+            back = sum_and_turn([[a_wide[t][:], clamped[t][:]] for t in range(PACK)], c0)
+            nc.scalar.copy(z_words[:, :, c0 // PACK : (c0 + HALF) // PACK, :], back[:].rearrange("p u (m t) -> p t m u", t=PACK))
+
+        both = keep.tile([P, PACK, HALF], F32, name="both", tag="step2")
+        for t in range(PACK):
+            nc.vector.tensor_tensor(both[:, t, :], b_rows[t][:].indirect(entries(n2_l, HALF, D)), b_last[t][:], ALU.add)
+        z2 = [quantise("z2_0", y_first[:], HALF)]
+        m3 = keep.tile([P, PACK, HALF], F32, name="m3")
+        for t in range(PACK):
+            nc.vector.tensor_tensor(m3[:, t, :], b_rows[t][:].indirect(entries(n3_l, HALF, D)), both[:, t, :], ALU.subtract)
+        m4 = keep.tile([P, PACK, HALF], F32, name="m4")
+        for t in range(PACK):
+            nc.vector.tensor_tensor(m4[:, t, :], b_rows[t][:].indirect(entries(n4_l, HALF, D)), both[:, t, :], ALU.subtract)
+        z = quantise("z", z_packed[:], D)
+
+        ds = [keep.tile([P, D], F32, name="ds%d" % t) for t in range(PACK)]
+        acc = psum.tile([P, D], F32, name="prod", tag="prod", bufs=2)
+        mx(acc[:, 0:HALF], z, 0, z2[0])
+        nc.scalar.activation(ds[0][:, 0:HALF], acc[:, 0:HALF], ACT.Copy, scale=S_SCALE)
+        y_last = []
+        for c in range(2):
+            cols = slice(P * c, P * (c + 1))
+            tile = keep.tile([P, PACK * P], BF16, name="y_last", tag=("z_packed", "y_first")[c], align_bytes=64)
+            nc.vector.tensor_tensor(
+                tile[:].rearrange("p (c i t) -> p c t i", t=PACK, i=4),
+                m3[:, :, cols].rearrange("p t (c i) -> p c t i", i=4), m4[:, :, cols].rearrange("p t (c i) -> p c t i", i=4), ALU.min,
+            )
+            y_last.append(tile)
+        for c in range(2):
+            z2.append(quantise("z2_%d" % (c + 1), y_last[c][:], P))
+            cols = slice(HALF + P * c, HALF + P * (c + 1))
+            mx(acc[:, cols], z, 0, z2[c + 1])
+            nc.scalar.activation(ds[0][:, cols], acc[:, cols], ACT.Copy, scale=-S_SCALE)
+        for t in range(1, PACK):
+            acc = psum.tile([P, D], F32, name="prod", tag="prod", bufs=2)
+            mx(acc[:, 0:HALF], z, t, z2[0])
+            mx(acc[:, HALF : HALF + P], z, t, z2[1])
+            mx(acc[:, HALF + P : D], z, t, z2[2])
+            nc.scalar.activation(ds[t][:, 0:HALF], acc[:, 0:HALF], ACT.Copy, scale=S_SCALE)
+            nc.scalar.activation(ds[t][:, LAST], acc[:, LAST], ACT.Copy, scale=-S_SCALE)
 
         pa = keep.tile([P, PACK, D // 2], F32, name="pa")
         pb = keep.tile([P, PACK, D // 2], F32, name="pb")

@@ -21,7 +21,6 @@ GROUP = 16
 HALF = D // 2
 FLOPS = 3 * 2 * D * D * D
 S_SCALE = 0.0625
-HALF_BIG = 2.0**126
 
 
 def tile_picked_kqbigtrimfoldd_none_po_kernel(
@@ -72,10 +71,10 @@ def tile_picked_kqbigtrimfoldd_none_po_kernel(
         gb_t = load_gain("gb_t", gb)
         n3_l = load_list("n3_l", n3)
         n4_l = load_list("n4_l", n4)
-        n2_l = load_list("n2_l", n2)
-        ga_t = load_gain("ga_t", ga)
         w1_raw = load_words("w1_raw", w1_words, D)
         load_plane(nc.sync, w1_plane, w1_scales)
+        n2_l = load_list("n2_l", n2)
+        ga_t = load_gain("ga_t", ga)
         n1_l = load_list("n1_l", n1)
         n5_l = load_list("n5_l", n5)
         n6_l = load_list("n6_l", n6)
@@ -123,10 +122,6 @@ def tile_picked_kqbigtrimfoldd_none_po_kernel(
             nc.scalar.activation(a_gain[:, t : t + 1], ga_t[:, t : t + 1], ACT.Copy, scale=flip[:, t : t + 1])
         a_sign = keep.tile([P, PACK], F32, name="a_sign")
         nc.scalar.activation(a_sign[:], a_gain[:], ACT.Sign)
-        a_low = keep.tile([P, PACK], F32, name="a_low")
-        nc.scalar.activation(a_low[:], a_sign[:], ACT.Copy, scale=HALF_BIG, bias=-HALF_BIG)
-        a_high = keep.tile([P, PACK], F32, name="a_high")
-        nc.scalar.activation(a_high[:], a_sign[:], ACT.Copy, scale=HALF_BIG, bias=HALF_BIG)
 
         two_plane = pick_plane("two_plane", two_l)
         offs_plane = pick_plane("offs_plane", offs_l)
@@ -150,7 +145,7 @@ def tile_picked_kqbigtrimfoldd_none_po_kernel(
             nc.scalar.activation(a_wide[t ^ 1][:, D : 2 * D], acc[:], ACT.Copy, scale=a_gain[:, t : t + 1])
         for t in range(PACK):
             last = keep.tile([P, HALF], F32, name="b_last%d" % t)
-            nc.scalar.copy(last[:], b_rows[t][:, LAST])
+            nc.sync.dma_start(last[:], b_rows[t][:, LAST])
             b_last.append(last)
 
         def sum_and_turn(terms, c0):
@@ -169,81 +164,83 @@ def tile_picked_kqbigtrimfoldd_none_po_kernel(
                     nc.tensor.transpose(back[:, u, P * c : P * (c + 1)], turned[:, u, :].bitcast(F32), ident[:])
             return back
 
-        def quantise(name, src, width):
-            codes = keep.tile([P, width], U32, name=name + "_codes", align_bytes=64)
+        def quantise(name, src, width, tag):
+            codes = keep.tile([P, width], U32, name=name + "_codes", tag=tag, align_bytes=64)
             scales = keep.tile([P, width], U8, name=name + "_scales", align_bytes=64)
             nc.vector.quantize_mx(out=codes[:].bitcast(FP8X4), scales=scales[:], in_=src)
             return codes, scales
 
-        g3_pairs = [keep.tile([P, 2, HALF], F32, name="g3", tag=tag, align_bytes=64) for tag in ("g3", "w1_plane")]
-        g3 = [g3_pairs[t // 2][:, t % 2, :] for t in range(PACK)]
-        d43 = keep.tile([P, PACK, HALF], F32, name="d43")
+        g3 = keep.tile([P, PACK, HALF], F32, name="g3")
+        d43 = keep.tile([P, PACK, HALF], F32, name="d43", tag="w1_plane", align_bytes=64)
         d23 = keep.tile([P, PACK, HALF], F32, name="d23")
         r34 = keep.tile([P, PACK, HALF], F32, name="r34")
         for t in range(PACK + 1):
             if t < PACK:
-                nc.vector.tensor_copy(g3[t], b_rows[t][:].indirect(entries(n3_l, 0, HALF)))
+                nc.vector.tensor_copy(g3[:, t, :], b_rows[t][:].indirect(entries(n3_l, 0, HALF)))
             if t > 0:
                 s = t - 1
-                nc.vector.tensor_tensor(d43[:, s, :], b_rows[s][:].indirect(entries(n4_l, 0, HALF)), g3[s], ALU.subtract)
+                nc.vector.tensor_tensor(d43[:, s, :], b_rows[s][:].indirect(entries(n4_l, 0, HALF)), g3[:, s, :], ALU.subtract)
                 nc.scalar.activation(r34[:, s, :], d43[:, s, :], ACT.Relu, scale=-1.0)
-                nc.vector.tensor_tensor(d23[:, s, :], b_rows[s][:].indirect(entries(n2_l, 0, HALF)), g3[s], ALU.subtract)
+                nc.vector.tensor_tensor(d23[:, s, :], b_rows[s][:].indirect(entries(n2_l, 0, HALF)), g3[:, s, :], ALU.subtract)
         back = sum_and_turn([[b_rows[t][:], r34[:, t, :], d23[:, t, :]] for t in range(PACK)], 0)
         y_first = keep.tile([P, PACK * HALF], BF16, name="y_first", tag="y_first", align_bytes=64)
         nc.scalar.copy(y_first[:].bitcast(F32).rearrange("p (j u) -> p j u", u=2), back[:].rearrange("p u j -> p j u"))
 
-        steps, clamped = [], []
-        for t in range(PACK + 1):
-            if t < PACK:
-                step = keep.tile([P, D], F32, name="step", tag="step%d" % t)
-                nc.vector.tensor_tensor(step[:], a_wide[t][:].indirect(n1_l[:]), a_wide[t ^ 1][:, D : 2 * D], ALU.subtract)
-                steps.append(step)
-            if t > 0:
-                s = t - 1
-                kept = keep.tile([P, D], F32, name="clamped%d" % s)
-                nc.vector.tensor_scalar(kept[:], steps[s][:], a_low[:, s : s + 1], a_high[:, s : s + 1], ALU.max, ALU.min)
-                clamped.append(kept)
-        z_packed = keep.tile([P, PACK * D], BF16, name="z_packed", tag="z_packed", align_bytes=64)
-        z_words = z_packed[:].bitcast(F32).rearrange("p (t m u) -> p t m u", t=PACK, u=2)
+        clamped = []
+        for t in range(PACK):
+            step = keep.tile([P, D], F32, name="step", tag="step%d" % t)
+            nc.vector.tensor_tensor(step[:], a_wide[t][:].indirect(n1_l[:]), a_wide[t ^ 1][:, D : 2 * D], ALU.subtract)
+            rise = keep.tile([P, D], F32, name="rise%d" % t)
+            nc.scalar.activation(rise[:], step[:], ACT.Relu, scale=a_sign[:, t : t + 1])
+            kept = keep.tile([P, D], F32, name="clamped%d" % t)
+            nc.scalar.activation(kept[:], rise[:], ACT.Copy, scale=a_sign[:, t : t + 1])
+            clamped.append(kept)
+        z_first = keep.tile([P, PACK * P], BF16, name="z_first", tag="z_first", align_bytes=64)
+        z_rest = keep.tile([P, (PACK - 1) * PACK * P], BF16, name="z_rest", align_bytes=64)
         for c0 in (0, HALF):
             back = sum_and_turn([[a_wide[t][:], clamped[t][:]] for t in range(PACK)], c0)
-            nc.scalar.copy(z_words[:, :, c0 // PACK : (c0 + HALF) // PACK, :], back[:].rearrange("p u (m t) -> p t m u", t=PACK))
+            dealt = back[:].rearrange("p u (m t) -> p t m u", t=PACK)
+            places = slice(c0 // PACK, (c0 + HALF) // PACK)
+            nc.scalar.copy(z_first[:].bitcast(F32).rearrange("p (m u) -> p m u", u=2)[:, places, :], dealt[:, 0])
+            nc.scalar.copy(z_rest[:].bitcast(F32).rearrange("p (t m u) -> p t m u", t=PACK - 1, u=2)[:, :, places, :], dealt[:, 1:PACK])
 
-        both = keep.tile([P, PACK, HALF], F32, name="both", tag="step2")
+        both = keep.tile([P, PACK, HALF], F32, name="both", tag="step1")
         for t in range(PACK):
             nc.vector.tensor_tensor(both[:, t, :], b_rows[t][:].indirect(entries(n2_l, HALF, D)), b_last[t][:], ALU.add)
-        z2 = [quantise("z2_0", y_first[:], HALF)]
+        z2 = [quantise("z2_0", y_first[:], HALF, "z2_0")]
         m3 = keep.tile([P, PACK, HALF], F32, name="m3")
         for t in range(PACK):
             nc.vector.tensor_tensor(m3[:, t, :], b_rows[t][:].indirect(entries(n3_l, HALF, D)), both[:, t, :], ALU.subtract)
         m4 = keep.tile([P, PACK, HALF], F32, name="m4")
         for t in range(PACK):
             nc.vector.tensor_tensor(m4[:, t, :], b_rows[t][:].indirect(entries(n4_l, HALF, D)), both[:, t, :], ALU.subtract)
-        z = quantise("z", z_packed[:], D)
+        z_0 = quantise("z_0", z_first[:], P, "z_0")
 
         ds = [keep.tile([P, D], F32, name="ds%d" % t) for t in range(PACK)]
         acc = psum.tile([P, D], F32, name="prod", tag="prod", bufs=2)
-        mx(acc[:, 0:HALF], z, 0, z2[0])
+        mx(acc[:, 0:HALF], z_0, 0, z2[0])
         nc.scalar.activation(ds[0][:, 0:HALF], acc[:, 0:HALF], ACT.Copy, scale=S_SCALE)
         y_last = []
         for c in range(2):
             cols = slice(P * c, P * (c + 1))
-            tile = keep.tile([P, PACK * P], BF16, name="y_last", tag=("z_packed", "y_first")[c], align_bytes=64)
+            tile = keep.tile([P, PACK * P], BF16, name="y_last", tag=("z_first", "y_first")[c], align_bytes=64)
             nc.vector.tensor_tensor(
                 tile[:].rearrange("p (c i t) -> p c t i", t=PACK, i=4),
                 m3[:, :, cols].rearrange("p t (c i) -> p c t i", i=4), m4[:, :, cols].rearrange("p t (c i) -> p c t i", i=4), ALU.min,
             )
             y_last.append(tile)
         for c in range(2):
-            z2.append(quantise("z2_%d" % (c + 1), y_last[c][:], P))
+            z2.append(quantise("z2_%d" % (c + 1), y_last[c][:], P, "z2_%d" % (c + 1)))
             cols = slice(HALF + P * c, HALF + P * (c + 1))
-            mx(acc[:, cols], z, 0, z2[c + 1])
+            mx(acc[:, cols], z_0, 0, z2[c + 1])
             nc.scalar.activation(ds[0][:, cols], acc[:, cols], ACT.Copy, scale=-S_SCALE)
-        for t in range(1, PACK):
+        z_1 = quantise("z_1", z_rest[:, 0 : PACK * P], P, "z_first")
+        z_23 = quantise("z_23", z_rest[:, PACK * P : 3 * PACK * P], 2 * P, "y_first")
+        for t, (lhs, i) in enumerate([(z_1, 0), (z_23, 0), (z_23, 1)], start=1):
             acc = psum.tile([P, D], F32, name="prod", tag="prod", bufs=2)
-            mx(acc[:, 0:HALF], z, t, z2[0])
-            mx(acc[:, HALF : HALF + P], z, t, z2[1])
-            mx(acc[:, HALF + P : D], z, t, z2[2])
+            mx(acc[:, 0:HALF], lhs, i, z2[0])
+            mx(acc[:, HALF : HALF + P], lhs, i, z2[1])
+            mx(acc[:, HALF + P : D], lhs, i, z2[2])
             nc.scalar.activation(ds[t][:, 0:HALF], acc[:, 0:HALF], ACT.Copy, scale=S_SCALE)
             nc.scalar.activation(ds[t][:, LAST], acc[:, LAST], ACT.Copy, scale=-S_SCALE)
 
@@ -265,32 +262,29 @@ def tile_picked_kqbigtrimfoldd_none_po_kernel(
         out_words = out_1[0].rearrange("p n t -> p (n t)").bitcast(I32)
         o_codes = keep.tile([P, D], U32, name="o_codes", align_bytes=64)
         o_plane = keep.tile([P, D], U8, name="o_plane", align_bytes=64)
-        chunks = [(0, 256), (256, 384), (384, 512)]
         results, packs = [], []
-        for c0, c1 in chunks:
-            width = c1 - c0
-            res = keep.tile([P, PACK, width], F32, name="res%d" % c0)
+        for c0 in (0, HALF):
+            res = keep.tile([P, PACK, HALF], F32, name="res%d" % c0)
             for t in range(PACK):
-                nc.vector.tensor_tensor(res[:, t, :], halves[t][:].indirect(entries(n7_l, c0, c1)), ds[t][:, c0:c1], ALU.add)
-            nc.sync.dma_start(out_rows[:, :, c0:c1], res[:])
+                nc.vector.tensor_tensor(res[:, t, :], halves[t][:].indirect(entries(n7_l, c0, c0 + HALF)), ds[t][:, c0 : c0 + HALF], ALU.add)
+                if t % 2 == 1:
+                    nc.sync.dma_start(out_rows[:, t - 1 : t + 1, c0 : c0 + HALF], res[:, t - 1 : t + 1, :])
             results.append(res)
-            if c1 < D:
-                packed = keep.tile([P, PACK * width], BF16, name="res_packed", tag="res_packed%d" % c0, align_bytes=64)
-                nc.scalar.copy(packed[:].rearrange("p (c i t) -> p c t i", t=PACK, i=4), res[:].rearrange("p t (c i) -> p c t i", i=4))
-                packs.append(packed)
+            packs.append(keep.tile([P, PACK * HALF], BF16, name="res_packed%d" % c0, align_bytes=64))
+
+        def interleave(copy, i, c0, c1):
+            copy(packs[i][:, PACK * c0 : PACK * c1].rearrange("p (c i t) -> p c t i", t=PACK, i=4), results[i][:, :, c0:c1].rearrange("p t (c i) -> p c t i", i=4))
 
         def quantise_out(i):
-            c0, c1 = chunks[i]
-            nc.vector.quantize_mx(out=o_codes[:, c0:c1].bitcast(FP8X4), scales=o_plane[:, c0:c1], in_=packs[i][:])
+            cols = slice(HALF * i, HALF * (i + 1))
+            nc.vector.quantize_mx(out=o_codes[:, cols].bitcast(FP8X4), scales=o_plane[:, cols], in_=packs[i][:])
+            nc.scalar.dma_start(out_words[:, cols], o_codes[:, cols].bitcast(I32))
 
+        interleave(nc.scalar.copy, 0, 0, HALF)
         quantise_out(0)
-        packed = keep.tile([P, PACK * P], BF16, name="res_packed", tag="res_packed0", align_bytes=64)
-        nc.vector.tensor_copy(packed[:].rearrange("p (c i t) -> p c t i", t=PACK, i=4), results[2][:].rearrange("p t (c i) -> p c t i", i=4))
-        packs.append(packed)
+        interleave(nc.scalar.copy, 1, 0, P)
+        interleave(nc.vector.tensor_copy, 1, P, HALF)
         quantise_out(1)
-        nc.sync.dma_start(out_words[:, 0:384], o_codes[:, 0:384].bitcast(I32))
-        quantise_out(2)
-        nc.scalar.dma_start(out_words[:, 384:512], o_codes[:, 384:512].bitcast(I32))
         for q in range(4):
             queue = nc.sync if q % 2 == 0 else nc.scalar
             queue.dma_start(out_2[0, 4 * q : 4 * q + 4, :].bitcast(I32), o_plane[32 * q : 32 * q + 4, :].bitcast(I32))

from contextlib import ExitStack

import concourse.mybir as mybir
from concourse.masks import make_identity

F32 = mybir.dt.float32
BF16 = mybir.dt.bfloat16
I32 = mybir.dt.int32
U32 = mybir.dt.uint32
U16 = mybir.dt.uint16
U8 = mybir.dt.uint8
FP8X4 = mybir.dt.float8_e4m3fn_x4
ALU = mybir.AluOpType
ACT = mybir.ActivationFunctionType

P = 128
PACK = 4
T = 2048
D = 512
GROUP = 16
HALF = D // 2
FLOPS = 3 * 2 * D * D * D
S_SCALE = 0.0625


def tile_picked_kqbigtrimfoldd_none_po_kernel(
    tc, x_words, x_scales, w1_words, w1_scales, w2_words, w2_scales, ga, gb, offs, two, n1, n2, n3, n4, n5, n6, n7, out_0, out_1, out_2
):
    nc = tc.nc
    with ExitStack() as ctx:
        keep = ctx.enter_context(tc.tile_pool(name="keep", bufs=1))
        psum = ctx.enter_context(tc.psum_pool(name="psum", bufs=1))

        def load_list(name, src):
            tile = keep.tile(list(src.shape), U16, name=name)
            nc.sync.dma_start(tile[:], src)
            return tile

        def entries(lst, c0, c1):
            return lst[:, c0 // GROUP : c1 // GROUP]

        def load_words(name, src, width):
            tile = keep.tile([P, width], I32, name=name, align_bytes=64)
            nc.sync.dma_start(tile[:], src[0].rearrange("p n t -> p (n t)").bitcast(I32))
            return tile

        def cleared_plane(name, width):
            tile = keep.tile([P, width], U8, name=name, tag=name, align_bytes=64)
            nc.vector.memset(tile[:, 0 : width // 2].bitcast(I32), 0)
            nc.gpsimd.memset(tile[:, width // 2 : width].bitcast(I32), 0)
            return tile

        def load_plane(queue, tile, src):
            for q in range(4):
                queue.dma_start(tile[32 * q : 32 * q + 4, :].bitcast(I32), src[0, 4 * q : 4 * q + 4, :].bitcast(I32))

        def load_gain(name, src):
            tile = keep.tile([P, PACK], F32, name=name)
            nc.sync.dma_start(tile[:], src.rearrange("(p t) o -> p (t o)", t=PACK))
            return tile

        x_plane = cleared_plane("x_plane", T)
        w2_plane = cleared_plane("w2_plane", D)
        w1_plane = cleared_plane("w1_plane", D)
        two_l = load_list("two_l", two)
        offs_l = load_list("offs_l", offs)
        w2_raw = load_words("w2_raw", w2_words, D)
        load_plane(nc.sync, x_plane, x_scales)
        x_codes = load_words("x_codes", x_words, T)
        load_plane(nc.sync, w2_plane, w2_scales)
        gb_t = load_gain("gb_t", gb)
        n3_l = load_list("n3_l", n3)
        n4_l = load_list("n4_l", n4)
        w1_raw = load_words("w1_raw", w1_words, D)
        load_plane(nc.sync, w1_plane, w1_scales)
        n2_l = load_list("n2_l", n2)
        ga_t = load_gain("ga_t", ga)
        n1_l = load_list("n1_l", n1)
        n5_l = load_list("n5_l", n5)
        n6_l = load_list("n6_l", n6)
        n7_l = load_list("n7_l", n7)

        ident = keep.tile([P, P], F32, name="ident")
        make_identity(nc, ident[:])

        def pick_plane(name, lst):
            tile = keep.tile([P, D], U8, name=name, align_bytes=64)
            nc.vector.tensor_copy(tile[:], x_plane[:].indirect(lst[:]))
            return tile

        def pick_codes(name, lst, tag):
            tile = keep.tile([P, D], U32, name=name, tag=tag, align_bytes=64)
            nc.vector.tensor_copy(tile[:], x_codes[:].bitcast(U32).indirect(lst[:]))
            return tile

        def deal(name, raw, plane):
            codes = keep.tile([P, D], I32, name=name + "_codes", align_bytes=64)
            nc.vector.tensor_copy(
                codes[:].rearrange("p (t m i) -> p m t i", t=PACK, i=4), raw[:].rearrange("p (m i t) -> p m t i", t=PACK, i=4)
            )
            scales = keep.tile([P, D], U8, name=name + "_scales", align_bytes=64)
            nc.vector.tensor_copy(
                scales[:].rearrange("p (t m i) -> p m t i", t=PACK, i=16), plane[:].rearrange("p (m i t) -> p m t i", t=PACK, i=16)
            )
            return codes, scales

        def mx(out, lhs, t, rhs):
            cols = slice(P * t, P * (t + 1))
            nc.tensor.matmul_mx(
                out=out, lhsT=lhs[0][:, cols].bitcast(FP8X4), lhsT_scale=lhs[1][:, cols],
                rhs=rhs[0][:].bitcast(FP8X4), rhs_scale=rhs[1][:], start=True, stop=True,
            )

        flip = keep.tile([P, PACK], F32, name="flip")
        nc.scalar.activation(flip[:], gb_t[:], ACT.Sign, scale=-1.0)
        gb_abs = keep.tile([P, PACK], F32, name="gb_abs")
        nc.scalar.activation(gb_abs[:], gb_t[:], ACT.Abs)
        b_gain = keep.tile([P, PACK], F32, name="b_gain")
        nc.scalar.activation(b_gain[:], gb_abs[:], ACT.Copy, scale=-1.0)
        a_gain = keep.tile([P, PACK], F32, name="a_gain")
        for t in range(PACK):
            nc.scalar.activation(a_gain[:, t : t + 1], ga_t[:, t : t + 1], ACT.Copy, scale=flip[:, t : t + 1])
        a_sign = keep.tile([P, PACK], F32, name="a_sign")
        nc.scalar.activation(a_sign[:], a_gain[:], ACT.Sign)

        two_plane = pick_plane("two_plane", two_l)
        offs_plane = pick_plane("offs_plane", offs_l)
        two_codes = pick_codes("two_codes", two_l, "two_codes")
        w2 = deal("w2", w2_raw, w2_plane)
        LAST = slice(HALF, D)
        b_rows, b_last = [], []
        for t in range(PACK):
            acc = psum.tile([P, D], F32, name="prod", tag="prod", bufs=2)
            mx(acc[:], w2, t, (two_codes, two_plane))
            row = keep.tile([P, D], F32, name="b_row%d" % t)
            nc.scalar.activation(row[:], acc[:], ACT.Copy, scale=b_gain[:, t : t + 1])
            b_rows.append(row)
        offs_codes = pick_codes("offs_codes", offs_l, "w2_plane")
        w1 = deal("w1", w1_raw, w1_plane)
        a_wide = [keep.tile([P, 2 * D], F32, name="a_wide%d" % t) for t in range(PACK)]
        for t in range(PACK):
            acc = psum.tile([P, D], F32, name="prod", tag="prod", bufs=2)
            mx(acc[:], w1, t, (offs_codes, offs_plane))
            nc.scalar.activation(a_wide[t][:, 0:D], acc[:], ACT.Copy, scale=a_gain[:, t : t + 1])
            nc.scalar.activation(a_wide[t ^ 1][:, D : 2 * D], acc[:], ACT.Copy, scale=a_gain[:, t : t + 1])
        for t in range(PACK):
            last = keep.tile([P, HALF], F32, name="b_last%d" % t)
            nc.sync.dma_start(last[:], b_rows[t][:, LAST])
            b_last.append(last)

        def sum_and_turn(terms, c0):
            back = psum.tile([P, 2, HALF], F32, name="back", tag="back", bufs=2)
            for c in range(HALF // P):
                cols = slice(c0 + P * c, c0 + P * (c + 1))
                total = psum.tile([P, PACK, P], F32, name="total", tag="total", bufs=4)
                for t in range(PACK):
                    for i, term in enumerate(terms[t]):
                        nc.tensor.matmul(total[:, t, :], term[:, cols], ident[:], start=(i == 0), stop=(i == len(terms[t]) - 1), is_transpose=True)
                turned = keep.tile([P, 2, 2 * P], BF16, name="turned", tag="turned", bufs=4)
                nc.scalar.activation(
                    turned[:].rearrange("j u (p e) -> j u p e", e=2), total[:].rearrange("j (u e) p -> j u p e", e=2), ACT.Copy
                )
                for u in range(2):
                    nc.tensor.transpose(back[:, u, P * c : P * (c + 1)], turned[:, u, :].bitcast(F32), ident[:])
            return back

        def quantise(name, src, width, tag):
            codes = keep.tile([P, width], U32, name=name + "_codes", tag=tag, align_bytes=64)
            scales = keep.tile([P, width], U8, name=name + "_scales", align_bytes=64)
            nc.vector.quantize_mx(out=codes[:].bitcast(FP8X4), scales=scales[:], in_=src)
            return codes, scales

        g3 = keep.tile([P, PACK, HALF], F32, name="g3")
        d43 = keep.tile([P, PACK, HALF], F32, name="d43", tag="w1_plane", align_bytes=64)
        d23 = keep.tile([P, PACK, HALF], F32, name="d23")
        r34 = keep.tile([P, PACK, HALF], F32, name="r34")
        for t in range(PACK + 1):
            if t < PACK:
                nc.vector.tensor_copy(g3[:, t, :], b_rows[t][:].indirect(entries(n3_l, 0, HALF)))
            if t > 0:
                s = t - 1
                nc.vector.tensor_tensor(d43[:, s, :], b_rows[s][:].indirect(entries(n4_l, 0, HALF)), g3[:, s, :], ALU.subtract)
                nc.scalar.activation(r34[:, s, :], d43[:, s, :], ACT.Relu, scale=-1.0)
                nc.vector.tensor_tensor(d23[:, s, :], b_rows[s][:].indirect(entries(n2_l, 0, HALF)), g3[:, s, :], ALU.subtract)
        back = sum_and_turn([[b_rows[t][:], r34[:, t, :], d23[:, t, :]] for t in range(PACK)], 0)
        y_first = keep.tile([P, PACK * HALF], BF16, name="y_first", tag="y_first", align_bytes=64)
        nc.scalar.copy(y_first[:].bitcast(F32).rearrange("p (j u) -> p j u", u=2), back[:].rearrange("p u j -> p j u"))

        clamped = []
        for t in range(PACK):
            step = keep.tile([P, D], F32, name="step", tag="step%d" % t)
            nc.vector.tensor_tensor(step[:], a_wide[t][:].indirect(n1_l[:]), a_wide[t ^ 1][:, D : 2 * D], ALU.subtract)
            rise = keep.tile([P, D], F32, name="rise%d" % t)
            nc.scalar.activation(rise[:], step[:], ACT.Relu, scale=a_sign[:, t : t + 1])
            kept = keep.tile([P, D], F32, name="clamped%d" % t)
            nc.scalar.activation(kept[:], rise[:], ACT.Copy, scale=a_sign[:, t : t + 1])
            clamped.append(kept)
        z_first = keep.tile([P, PACK * P], BF16, name="z_first", tag="z_first", align_bytes=64)
        z_rest = keep.tile([P, (PACK - 1) * PACK * P], BF16, name="z_rest", align_bytes=64)
        for c0 in (0, HALF):
            back = sum_and_turn([[a_wide[t][:], clamped[t][:]] for t in range(PACK)], c0)
            dealt = back[:].rearrange("p u (m t) -> p t m u", t=PACK)
            places = slice(c0 // PACK, (c0 + HALF) // PACK)
            nc.scalar.copy(z_first[:].bitcast(F32).rearrange("p (m u) -> p m u", u=2)[:, places, :], dealt[:, 0])
            nc.scalar.copy(z_rest[:].bitcast(F32).rearrange("p (t m u) -> p t m u", t=PACK - 1, u=2)[:, :, places, :], dealt[:, 1:PACK])

        both = keep.tile([P, PACK, HALF], F32, name="both", tag="step1")
        for t in range(PACK):
            nc.vector.tensor_tensor(both[:, t, :], b_rows[t][:].indirect(entries(n2_l, HALF, D)), b_last[t][:], ALU.add)
        z2 = [quantise("z2_0", y_first[:], HALF, "z2_0")]
        m3 = keep.tile([P, PACK, HALF], F32, name="m3")
        for t in range(PACK):
            nc.vector.tensor_tensor(m3[:, t, :], b_rows[t][:].indirect(entries(n3_l, HALF, D)), both[:, t, :], ALU.subtract)
        m4 = keep.tile([P, PACK, HALF], F32, name="m4")
        for t in range(PACK):
            nc.vector.tensor_tensor(m4[:, t, :], b_rows[t][:].indirect(entries(n4_l, HALF, D)), both[:, t, :], ALU.subtract)
        z_0 = quantise("z_0", z_first[:], P, "z_0")

        ds = [keep.tile([P, D], F32, name="ds%d" % t) for t in range(PACK)]
        acc = psum.tile([P, D], F32, name="prod", tag="prod", bufs=2)
        mx(acc[:, 0:HALF], z_0, 0, z2[0])
        nc.scalar.activation(ds[0][:, 0:HALF], acc[:, 0:HALF], ACT.Copy, scale=S_SCALE)
        y_last = []
        for c in range(2):
            cols = slice(P * c, P * (c + 1))
            tile = keep.tile([P, PACK * P], BF16, name="y_last", tag=("z_first", "y_first")[c], align_bytes=64)
            nc.vector.tensor_tensor(
                tile[:].rearrange("p (c i t) -> p c t i", t=PACK, i=4),
                m3[:, :, cols].rearrange("p t (c i) -> p c t i", i=4), m4[:, :, cols].rearrange("p t (c i) -> p c t i", i=4), ALU.min,
            )
            y_last.append(tile)
        for c in range(2):
            z2.append(quantise("z2_%d" % (c + 1), y_last[c][:], P, "z2_%d" % (c + 1)))
            cols = slice(HALF + P * c, HALF + P * (c + 1))
            mx(acc[:, cols], z_0, 0, z2[c + 1])
            nc.scalar.activation(ds[0][:, cols], acc[:, cols], ACT.Copy, scale=-S_SCALE)
        z_1 = quantise("z_1", z_rest[:, 0 : PACK * P], P, "z_first")
        z_23 = quantise("z_23", z_rest[:, PACK * P : 3 * PACK * P], 2 * P, "y_first")
        for t, (lhs, i) in enumerate([(z_1, 0), (z_23, 0), (z_23, 1)], start=1):
            acc = psum.tile([P, D], F32, name="prod", tag="prod", bufs=2)
            mx(acc[:, 0:HALF], lhs, i, z2[0])
            mx(acc[:, HALF : HALF + P], lhs, i, z2[1])
            mx(acc[:, HALF + P : D], lhs, i, z2[2])
            nc.scalar.activation(ds[t][:, 0:HALF], acc[:, 0:HALF], ACT.Copy, scale=S_SCALE)
            nc.scalar.activation(ds[t][:, LAST], acc[:, LAST], ACT.Copy, scale=-S_SCALE)

        pa = keep.tile([P, PACK, D // 2], F32, name="pa")
        pb = keep.tile([P, PACK, D // 2], F32, name="pb")
        halves = []
        for t in range(PACK + 1):
            if t < PACK:
                nc.vector.tensor_copy(pa[:, t, :], ds[t][:].indirect(n5_l[:]))
                nc.vector.tensor_scalar(pb[:, t, :], ds[t][:].indirect(n6_l[:]), -0.5, 0.0, ALU.mult, ALU.add)
            if t > 0:
                s = t - 1
                nc.vector.tensor_tensor(ds[s][:].indirect(n6_l[:]), pa[:, s, :], pb[:, s, :], ALU.add)
                half = keep.tile([P, D], F32, name="half%d" % s)
                nc.scalar.activation(half[:], ds[s][:], ACT.Copy, scale=-0.5)
                halves.append(half)

        out_rows = out_0.rearrange("(p t) v -> p t v", t=PACK)
        out_words = out_1[0].rearrange("p n t -> p (n t)").bitcast(I32)
        o_codes = keep.tile([P, D], U32, name="o_codes", align_bytes=64)
        o_plane = keep.tile([P, D], U8, name="o_plane", align_bytes=64)
        results, packs = [], []
        for c0 in (0, HALF):
            res = keep.tile([P, PACK, HALF], F32, name="res%d" % c0)
            for t in range(PACK):
                nc.vector.tensor_tensor(res[:, t, :], halves[t][:].indirect(entries(n7_l, c0, c0 + HALF)), ds[t][:, c0 : c0 + HALF], ALU.add)
                if t % 2 == 1:
                    nc.sync.dma_start(out_rows[:, t - 1 : t + 1, c0 : c0 + HALF], res[:, t - 1 : t + 1, :])
            results.append(res)
            packs.append(keep.tile([P, PACK * HALF], BF16, name="res_packed%d" % c0, align_bytes=64))

        def interleave(copy, i, c0, c1):
            copy(packs[i][:, PACK * c0 : PACK * c1].rearrange("p (c i t) -> p c t i", t=PACK, i=4), results[i][:, :, c0:c1].rearrange("p t (c i) -> p c t i", i=4))

        def quantise_out(i):
            cols = slice(HALF * i, HALF * (i + 1))
            nc.vector.quantize_mx(out=o_codes[:, cols].bitcast(FP8X4), scales=o_plane[:, cols], in_=packs[i][:])
            nc.scalar.dma_start(out_words[:, cols], o_codes[:, cols].bitcast(I32))

        interleave(nc.scalar.copy, 0, 0, HALF)
        quantise_out(0)
        interleave(nc.scalar.copy, 1, 0, P)
        interleave(nc.vector.tensor_copy, 1, P, HALF)
        quantise_out(1)
        for q in range(4):
            queue = nc.sync if q % 2 == 0 else nc.scalar
            queue.dma_start(out_2[0, 4 * q : 4 * q + 4, :].bitcast(I32), o_plane[32 * q : 32 * q + 4, :].bitcast(I32))
